import numpy as np
import ml_dtypes


def mxq(x, axis, fmt="e4m3"):
    dtype, down = {"e4m3": (ml_dtypes.float8_e4m3fn, 7), "e5m2": (ml_dtypes.float8_e5m2, 14)}[fmt]
    v = np.moveaxis(np.asarray(x, np.float32).astype(ml_dtypes.bfloat16).astype(np.float64), axis, -1)
    blocks = v.reshape(v.shape[:-1] + (-1, 32))
    amax = np.abs(blocks).max(-1, keepdims=True)
    byte = np.maximum(np.where(amax > 0, np.frexp(amax)[1] - 1 + 127, 0) - down, 1)
    scale = np.exp2(byte - 127.0)
    codes = (blocks / scale).astype(np.float32).astype(dtype).astype(np.float64)
    return np.moveaxis((codes * scale).reshape(v.shape), -1, axis)


WIDE = False


def mx_kscale(k):
    if not WIDE:
        return np.ones(k)
    levels = np.array([10, -10, 5, -5, 0])
    if k % 512:
        return np.exp2(np.random.permutation(np.resize(levels, k // 32))).repeat(32)
    a = np.empty((k // 512, 16))
    for p in range(k // 512):
        a[p, :8] = np.random.permutation(np.resize(levels, 8))
        for g in range(8):
            far = levels[np.abs(levels - a[p, g]) >= 10]
            a[p, g + 8] = far[np.random.randint(len(far))]
    return np.exp2(a.ravel()).repeat(32)


def f64(x):
    return np.asarray(x).astype(np.float64)


def striped(idx):
    return np.tile(idx.reshape(-1, 16).T, (8, 1)).astype(np.uint16)


def unstriped(offs):
    return offs[:16].T.reshape(-1).astype(np.int64)


E2M1 = np.array([0.0, 0.5, 1.0, 1.5, 2.0, 3.0, 4.0, 6.0, -0.0, -0.5, -1.0, -1.5, -2.0, -3.0, -4.0, -6.0])


def pack_weight(w, fmt):
    k, n = w.shape
    w = f64(np.asarray(w, np.float32).astype(ml_dtypes.bfloat16)).reshape(k // 32, 32, n)
    amax = np.abs(w).max(1)
    if fmt == "e4m3":
        byte = np.frexp(amax)[1] - 1 + 127 - 7
    else:
        mant, ex = np.frexp(amax / 6.0)
        byte = np.where(mant > 0.5, ex, ex - 1) + 127
    byte = np.clip(np.where(amax > 0, byte, 1), 1, 254)
    scaled = (w * np.exp2(127.0 - byte)[:, None, :]).reshape(k, n).astype(np.float32)
    by_word = np.ascontiguousarray(scaled.reshape(k // 512, 128, 4, n).transpose(0, 1, 3, 2))
    if fmt == "e4m3":
        words = by_word.astype(ml_dtypes.float8_e4m3fn).view(np.uint8)
    else:
        c = by_word.astype(ml_dtypes.float4_e2m1fn).view(np.uint8) & 0xF
        words = (c[..., 0::2] | (c[..., 1::2] << 4)).reshape(k // 512, 128, 2 * n)
    return np.ascontiguousarray(words), np.ascontiguousarray(byte.astype(np.uint8).reshape(k // 512, 16, n))


def unpack_weight(words, scales, fmt):
    g, _, n = scales.shape
    words = np.ascontiguousarray(words).reshape(g, 128, n, -1)
    if fmt == "e4m3":
        vals = words.view(ml_dtypes.float8_e4m3fn).astype(np.float64)
    else:
        nib = np.empty((g, 128, n, 4), np.uint8)
        nib[..., 0::2] = words & 0xF
        nib[..., 1::2] = words >> 4
        vals = E2M1[nib]
    vals = vals * np.repeat(np.exp2(scales.astype(np.float64) - 127.0), 8, axis=1)[..., None]
    return vals.transpose(0, 1, 3, 2).reshape(g * 512, n)


def gelu(v):
    return 0.5 * v * (1.0 + np.tanh(np.sqrt(2.0 / np.pi) * (v + 0.044715 * v**3)))


K, T, S, H, N = 1024, 2048, 1024, 512, 256

def setup_inputs():
    n = np.random.standard_normal
    s = mx_kscale(K)[:, None]
    u = mx_kscale(H)[:, None]
    tab_words, tab_scales = pack_weight(n((K, T)) * s, "e4m3")
    w2_words, w2_scales = pack_weight(n((K, H)) / np.sqrt(K) / s, "e4m3")
    w3_words, w3_scales = pack_weight(n((K, H)) / np.sqrt(K) / s, "e2m1")
    return {
        "tab_words": tab_words, "tab_scales": tab_scales,
        "offs": striped(np.random.permutation(T)[:S]),
        "offs2": striped(np.random.permutation(T)[:S]),
        "offs3": striped(np.random.permutation(T)[:S]),
        "w1": (n((K, H)) / np.sqrt(K) / s).astype(np.float32),
        "w2_words": w2_words, "w2_scales": w2_scales,
        "w3_words": w3_words, "w3_scales": w3_scales,
        "gain": (np.exp(0.3 * n(H)) * u[:, 0]).astype(np.float32),
        "w4": (2 * n((H, N)) / np.sqrt(H) / u).astype(np.float32),
        "b": (0.5 * n(N)).astype(np.float32),
    }

def reference(tab_words, tab_scales, offs, offs2, offs3, w1, w2_words, w2_scales, w3_words, w3_scales, gain, w4, b):
    v = unpack_weight(tab_words, tab_scales, "e4m3")
    v1 = v[:, unstriped(offs)]
    v2 = v[:, unstriped(offs2)]
    v3 = v[:, unstriped(offs3)]
    p1 = mxq(f64(w1), 0, "e4m3").T @ v1
    p2 = unpack_weight(w2_words, w2_scales, "e4m3").T @ v2
    p3 = unpack_weight(w3_words, w3_scales, "e2m1").T @ v3
    q = 1.0 / (1.0 + np.exp(-(p1 * p2 * p3)))
    h = q * f64(gain)[:, None]
    y = mxq(f64(w4), 0, "e4m3").T @ mxq(h, 0, "e4m3")
    return y + f64(b)[:, None]

@@ -1,0 +1,255 @@
+from contextlib import ExitStack
+
+import concourse.mybir as mybir
+
+K, T, S, H, N = 1024, 2048, 1024, 512, 256
+FLOPS = 2 * 3 * K * H * S + 2 * H * N * S
+
+F32 = mybir.dt.float32
+BF16 = mybir.dt.bfloat16
+I32 = mybir.dt.int32
+U32 = mybir.dt.uint32
+U16 = mybir.dt.uint16
+U8 = mybir.dt.uint8
+FP8X4 = mybir.dt.float8_e4m3fn_x4
+FP4X4 = mybir.dt.float4_e2m1fn_x4
+ACT = mybir.ActivationFunctionType
+MULT = mybir.AluOpType.mult
+
+P = 128
+PASSES = 2
+UNIT = 128
+CHUNK = 256
+CHUNKS = S // CHUNK
+
+
+def tile_list_polypharmacy_triple_risk_kernel(
+    tc, tab_words, tab_scales, offs, offs2, offs3, w1, w2_words, w2_scales, w3_words, w3_scales, gain, w4, b, out
+):
+    nc = tc.nc
+    with ExitStack() as ctx:
+        keep = ctx.enter_context(tc.tile_pool(name="keep", bufs=1))
+        ring = ctx.enter_context(tc.tile_pool(name="ring", bufs=2))
+        psum = ctx.enter_context(tc.psum_pool(name="psum", bufs=2))
+
+        lists = {}
+        for role in (2, 3, 1):
+            lists[role] = keep.tile([P, S // 16], U16, name="list%d" % role)
+        tab_plane = keep.tile([P, T], U8, align_bytes=64)
+        w_planes_raw = keep.tile([P, 3, H], U8, align_bytes=64)
+        v3_plane1 = keep.tile([P, S], U8, align_bytes=64)
+        warm = keep.tile([P, 2], F32)
+
+        nc.vector.memset(tab_plane[:].bitcast(I32), 0)
+        nc.gpsimd.memset(w_planes_raw[:].rearrange("p s c -> p (s c)").bitcast(I32), 0)
+        nc.gpsimd.memset(v3_plane1[:].bitcast(I32), 0)
+        nc.gpsimd.memset(warm[:, 0:1], 0.0)
+        nc.scalar.activation(out=warm[:, 1:2], in_=warm[:, 0:1], func=ACT.Sigmoid)
+
+        nc.sync.dma_start(lists[2][:], offs2)
+        nc.sync.dma_start(lists[3][:], offs3)
+        nc.sync.dma_start(lists[1][:], offs)
+        for q in range(4):
+            nc.sync.dma_start(
+                out=tab_plane[32 * q : 32 * q + 8, :].bitcast(I32),
+                in_=tab_scales[:, 4 * q : 4 * q + 4, :].bitcast(I32),
+            )
+        w1_raw = [keep.tile([P, 4, H], F32, name="w1_raw%d" % a) for a in range(PASSES)]
+        nc.sync.dma_start(out=w1_raw[0][:], in_=w1[0:512, :].rearrange("(p i) c -> p i c", i=4))
+        for q in range(4):
+            nc.sync.dma_start(
+                out=w_planes_raw[32 * q : 32 * q + 8, 0, :].bitcast(I32),
+                in_=w2_scales[:, 4 * q : 4 * q + 4, :].bitcast(I32),
+            )
+        nc.sync.dma_start(out=w1_raw[1][:], in_=w1[512:1024, :].rearrange("(p i) c -> p i c", i=4))
+        w2_raw = keep.tile([P, PASSES, H], I32)
+        nc.sync.dma_start(out=w2_raw[:], in_=w2_words.rearrange("a p c i -> p a (c i)").bitcast(I32))
+        w3_raw = keep.tile([P, PASSES, H // 2], I32)
+        nc.sync.dma_start(out=w3_raw[:], in_=w3_words.rearrange("a p c -> p a c").bitcast(I32))
+        for q in range(4):
+            nc.sync.dma_start(
+                out=w_planes_raw[32 * q : 32 * q + 4, 1:3, :].bitcast(I32),
+                in_=w3_scales[:, 4 * q : 4 * q + 4, :].rearrange("a r c -> r a c").bitcast(I32),
+            )
+        tab = [keep.tile([P, T], I32, name="tab%d" % a, align_bytes=64) for a in range(PASSES)]
+        for a in range(PASSES):
+            nc.sync.dma_start(out=tab[a][:], in_=tab_words[a].rearrange("p t i -> p (t i)").bitcast(I32))
+
+        v_plane = {}
+        for role in (2, 3, 1):
+            v_plane[role] = keep.tile([P, S], U8, name="v_plane%d" % role, align_bytes=64)
+            nc.vector.tensor_copy(v_plane[role][:], tab_plane[:].indirect(lists[role][:]))
+            if role == 3:
+                nc.sync.dma_start(out=v3_plane1[0 : P - 4, :].bitcast(I32), in_=v_plane[3][4:P, :].bitcast(I32))
+
+        w4_raw = keep.tile([P, 4, N], F32)
+        w4_rows = w4.rearrange("(u t e) n -> t u e n", t=4, e=4)
+        for t in range(4):
+            nc.sync.dma_start(out=w4_raw[:, t, :], in_=w4_rows[t])
+        gain_sb = keep.tile([P, 4], F32)
+        b_sb = keep.tile([P, 2], F32)
+        with nc.allow_non_contiguous_dma(reason="one value of a short vector for each partition"):
+            for e in range(4):
+                nc.sync.dma_start(out=gain_sb[e:P:4, :], in_=gain.rearrange("(u t e) -> e u t", t=4, e=4)[e])
+            nc.sync.dma_start(out=b_sb[:], in_=b.rearrange("(g p) -> p g", p=P))
+
+        w1_codes = keep.tile([P, PASSES, H], U32, align_bytes=64)
+        w1_planes = keep.tile([P, PASSES, H], U8, align_bytes=64)
+        for a in range(PASSES):
+            w1_bf = keep.tile([P, 4 * H], BF16, name="w1_bf%d" % a, align_bytes=64)
+            nc.scalar.copy(
+                out=w1_bf[:].rearrange("p (t u e i) -> p t u i e", t=4, e=4, i=4),
+                in_=w1_raw[a][:].rearrange("p i (u t e) -> p t u i e", t=4, e=4),
+            )
+            nc.vector.quantize_mx(out=w1_codes[:, a, :].bitcast(FP8X4), scales=w1_planes[:, a, :], in_=w1_bf[:])
+
+        w2_codes = keep.tile([P, PASSES, H], I32, align_bytes=64)
+        nc.vector.tensor_copy(
+            out=w2_codes[:].rearrange("p a (t u e) -> p a t u e", t=4, e=4),
+            in_=w2_raw[:].rearrange("p a (u t e) -> p a t u e", t=4, e=4),
+        )
+        w3_codes = keep.tile([P, PASSES, H // 2], I32, align_bytes=64)
+        nc.vector.tensor_copy(
+            out=w3_codes[:].rearrange("p a (t u e) -> p a t u e", t=4, e=2),
+            in_=w3_raw[:].rearrange("p a (u t e) -> p a t u e", t=4, e=2),
+        )
+        w_planes = keep.tile([P, 3, H], U8, align_bytes=64)
+        nc.vector.tensor_copy(
+            out=w_planes[:].bitcast(I32).rearrange("p s (t u) -> p s t u", t=4),
+            in_=w_planes_raw[:].bitcast(I32).rearrange("p s (u t) -> p s t u", t=4),
+        )
+
+        w4_bf = keep.tile([P, 4 * N], BF16, align_bytes=64)
+        nc.scalar.copy(
+            out=w4_bf[:].rearrange("p (c i t) -> p c t i", i=4, t=4),
+            in_=w4_raw[:].rearrange("p t (c i) -> p c t i", i=4),
+        )
+        w4_codes = keep.tile([P, N], U32, align_bytes=64)
+        w4_plane = keep.tile([P, N], U8, align_bytes=64)
+
+        def stationary(role, a, t):
+            cols = slice(P * t, P * t + P)
+            if role == 1:
+                return w1_codes[:, a, cols].bitcast(FP8X4), w1_planes[:, a, cols]
+            if role == 2:
+                return w2_codes[:, a, cols].bitcast(FP8X4), w_planes[4 * a : P, 0, cols]
+            return w3_codes[:, a, 64 * t : 64 * t + 64].bitcast(FP4X4), w_planes[:, 1 + a, cols]
+
+        def moving_plane(role, a, cols):
+            if role == 3 and a == 1:
+                return v3_plane1[:, cols]
+            return v_plane[role][4 * a : P, cols]
+
+        words = {}
+
+        def gather(c, role, a):
+            g = keep.tile([P, CHUNK], U32, name="g%d%d" % (role, a), align_bytes=64)
+            part = lists[role][:, c * CHUNK // 16 : (c + 1) * CHUNK // 16]
+            nc.vector.tensor_copy(g[:], tab[a][:].bitcast(U32).indirect(part))
+            words[(c, role, a)] = g
+
+        def project(role, unit):
+            c, half = divmod(unit, 2)
+            bank = psum.tile([P, 4, UNIT], F32, name="p%d" % role)
+            for t in range(4):
+                for a in range(PASSES):
+                    codes, plane = stationary(role, a, t)
+                    nc.tensor.matmul_mx(
+                        out=bank[:, t, :],
+                        lhsT=codes,
+                        lhsT_scale=plane,
+                        rhs=words[(c, role, a)][:, half * UNIT : (half + 1) * UNIT].bitcast(FP8X4),
+                        rhs_scale=moving_plane(role, a, slice(unit * UNIT, (unit + 1) * UNIT)),
+                        start=(a == 0),
+                        stop=(a == PASSES - 1),
+                    )
+            if c == CHUNKS - 1:
+                return bank[:].rearrange("p t j -> p j t")
+            return bank[:]
+
+        def shaped(flat, c):
+            if c == CHUNKS - 1:
+                return flat[:].rearrange("p (j t) -> p j t", t=4)
+            return flat[:].rearrange("p (t j) -> p t j", t=4)
+
+        def readout(h_bf, c):
+            h_codes = ring.tile([P, CHUNK], U32, name="h_codes", align_bytes=64)
+            h_plane = ring.tile([P, CHUNK], U8, name="h_plane", align_bytes=64)
+            nc.vector.quantize_mx(out=h_codes[:].bitcast(FP8X4), scales=h_plane[:], in_=h_bf[:])
+            for g in range(2):
+                y = psum.tile([P, CHUNK], F32, name="y")
+                nc.tensor.matmul_mx(
+                    out=y[:],
+                    lhsT=w4_codes[:, g * P : (g + 1) * P].bitcast(FP8X4),
+                    lhsT_scale=w4_plane[:, g * P : (g + 1) * P],
+                    rhs=h_codes[:].bitcast(FP8X4),
+                    rhs_scale=h_plane[:],
+                    start=True,
+                    stop=True,
+                )
+                res = ring.tile([P, CHUNK], F32, name="res%d" % g)
+                if c == CHUNKS - 1 and g == 1:
+                    nc.vector.tensor_scalar_add(out=res[:], in0=y[:], scalar1=b_sb[:, g : g + 1])
+                else:
+                    nc.scalar.activation(out=res[:], in_=y[:], func=ACT.Identity, bias=b_sb[:, g : g + 1])
+                nc.sync.dma_start(out=out[g * P : (g + 1) * P, c * CHUNK : (c + 1) * CHUNK], in_=res[:])
+
+        for a in range(PASSES):
+            for role in (2, 3, 1):
+                gather(0, role, a)
+        pending = None
+        for c in range(CHUNKS):
+            last = c == CHUNKS - 1
+            units = (2 * c, 2 * c + 1)
+            p2_sb, p23, x = {}, {}, {}
+            for unit in units:
+                p2 = project(2, unit)
+                p2_sb[unit] = ring.tile([P, 4 * UNIT], F32, name="p2_sb")
+                nc.scalar.copy(out=shaped(p2_sb[unit], c), in_=p2)
+            if not last:
+                for a in range(PASSES):
+                    gather(c + 1, 2, a)
+            for unit in units:
+                p3 = project(3, unit)
+                p23[unit] = ring.tile([P, 4 * UNIT], F32, name="p23")
+                nc.vector.tensor_tensor(out=shaped(p23[unit], c), in0=shaped(p2_sb[unit], c), in1=p3, op=MULT)
+            if not last:
+                for a in range(PASSES):
+                    gather(c + 1, 3, a)
+            if c == 0:
+                nc.vector.quantize_mx(out=w4_codes[:].bitcast(FP8X4), scales=w4_plane[:], in_=w4_bf[:])
+            if pending is not None:
+                readout(*pending)
+            for unit in units:
+                p1 = project(1, unit)
+                x[unit] = ring.tile([P, 4 * UNIT], F32, name="x")
+                nc.vector.tensor_tensor(out=shaped(x[unit], c), in0=shaped(p23[unit], c), in1=p1, op=MULT)
+            if not last:
+                for a in range(PASSES):
+                    gather(c + 1, 1, a)
+                sig = ring.tile([P, 4, CHUNK], F32, name="sig")
+                for half in range(2):
+                    nc.scalar.activation(
+                        out=sig[:, :, half * UNIT : (half + 1) * UNIT], in_=shaped(x[units[half]], c), func=ACT.Sigmoid
+                    )
+                h_rows = ring.tile([P, 4, CHUNK], BF16, name="h_rows")
+                for t in range(4):
+                    nc.scalar.activation(out=h_rows[:, t, :], in_=sig[:, t, :], func=ACT.Copy, scale=gain_sb[:, t : t + 1])
+                h_bf = ring.tile([P, 4 * CHUNK], BF16, name="h_bf", align_bytes=64)
+                nc.scalar.copy(
+                    out=h_bf[:].rearrange("p (c i t) -> p c t i", i=4, t=4),
+                    in_=h_rows[:].rearrange("p t (c i) -> p c t i", i=4),
+                )
+                pending = (h_bf, c)
+            else:
+                h_bf = ring.tile([P, 4 * CHUNK], BF16, name="h_bf", align_bytes=64)
+                for half in range(2):
+                    sig = ring.tile([P, UNIT, 4], F32, name="sig_last")
+                    nc.scalar.activation(out=sig[:], in_=shaped(x[units[half]], c), func=ACT.Sigmoid)
+                    nc.vector.tensor_tensor(
+                        out=h_bf[:, half * 4 * UNIT : (half + 1) * 4 * UNIT].rearrange("p (j t) -> p j t", t=4),
+                        in0=sig[:],
+                        in1=gain_sb[:].unsqueeze(1).to_broadcast([P, UNIT, 4]),
+                        op=MULT,
+                    )
+                readout(h_bf, c)

@@ -98,8 +98,8 @@ def tile_list_polypharmacy_triple_risk_kernel(
         for a in range(PASSES):
             w1_bf = keep.tile([P, 4 * H], BF16, name="w1_bf%d" % a, align_bytes=64)
             nc.scalar.copy(
-                out=w1_bf[:].rearrange("p (t u e i) -> p t u i e", t=4, e=4, i=4),
-                in_=w1_raw[a][:].rearrange("p i (u t e) -> p t u i e", t=4, e=4),
+                out=w1_bf[:].rearrange("p (t u e i) -> p t u e i", t=4, e=4, i=4),
+                in_=w1_raw[a][:].rearrange("p i (u t e) -> p t u e i", t=4, e=4),
             )
             nc.vector.quantize_mx(out=w1_codes[:, a, :].bitcast(FP8X4), scales=w1_planes[:, a, :], in_=w1_bf[:])
 
@@ -121,8 +121,8 @@ def tile_list_polypharmacy_triple_risk_kernel(
 
         w4_bf = keep.tile([P, 4 * N], BF16, align_bytes=64)
         nc.scalar.copy(
-            out=w4_bf[:].rearrange("p (c i t) -> p c t i", i=4, t=4),
-            in_=w4_raw[:].rearrange("p t (c i) -> p c t i", i=4),
+            out=w4_bf[:].rearrange("p (c t) -> p c t", t=4),
+            in_=w4_raw[:].rearrange("p t c -> p c t"),
         )
         w4_codes = keep.tile([P, N], U32, align_bytes=64)
         w4_plane = keep.tile([P, N], U8, align_bytes=64)
@@ -197,15 +197,20 @@ def tile_list_polypharmacy_triple_risk_kernel(
         for a in range(PASSES):
             for role in (2, 3, 1):
                 gather(0, role, a)
+        p2_sb = {}
+
+        def second_drug(c):
+            for unit in (2 * c, 2 * c + 1):
+                p2 = project(2, unit)
+                p2_sb[unit] = ring.tile([P, 4 * UNIT], F32, name="p2_sb")
+                nc.scalar.copy(out=shaped(p2_sb[unit], c), in_=p2)
+
+        second_drug(0)
         pending = None
         for c in range(CHUNKS):
             last = c == CHUNKS - 1
             units = (2 * c, 2 * c + 1)
-            p2_sb, p23, x = {}, {}, {}
-            for unit in units:
-                p2 = project(2, unit)
-                p2_sb[unit] = ring.tile([P, 4 * UNIT], F32, name="p2_sb")
-                nc.scalar.copy(out=shaped(p2_sb[unit], c), in_=p2)
+            p23, x = {}, {}
             if not last:
                 for a in range(PASSES):
                     gather(c + 1, 2, a)
@@ -214,6 +219,7 @@ def tile_list_polypharmacy_triple_risk_kernel(
                 p23[unit] = ring.tile([P, 4 * UNIT], F32, name="p23")
                 nc.vector.tensor_tensor(out=shaped(p23[unit], c), in0=shaped(p2_sb[unit], c), in1=p3, op=MULT)
             if not last:
+                second_drug(c + 1)
                 for a in range(PASSES):
                     gather(c + 1, 3, a)
             if c == 0:
@@ -237,8 +243,8 @@ def tile_list_polypharmacy_triple_risk_kernel(
                     nc.scalar.activation(out=h_rows[:, t, :], in_=sig[:, t, :], func=ACT.Copy, scale=gain_sb[:, t : t + 1])
                 h_bf = ring.tile([P, 4 * CHUNK], BF16, name="h_bf", align_bytes=64)
                 nc.scalar.copy(
-                    out=h_bf[:].rearrange("p (c i t) -> p c t i", i=4, t=4),
-                    in_=h_rows[:].rearrange("p t (c i) -> p c t i", i=4),
+                    out=h_bf[:].rearrange("p (c t) -> p c t", t=4),
+                    in_=h_rows[:].rearrange("p t c -> p c t"),
                 )
                 pending = (h_bf, c)
             else:

@@ -40,20 +40,20 @@ def tile_list_polypharmacy_triple_risk_kernel(
         v3_plane1 = keep.tile([P, S], U8, align_bytes=64)
         warm = keep.tile([P, 2], F32)
 
-        nc.vector.memset(tab_plane[:].bitcast(I32), 0)
+        nc.gpsimd.memset(tab_plane[:].bitcast(I32), 0)
         nc.gpsimd.memset(w_planes_raw[:].rearrange("p s c -> p (s c)").bitcast(I32), 0)
         nc.gpsimd.memset(v3_plane1[:].bitcast(I32), 0)
         nc.gpsimd.memset(warm[:, 0:1], 0.0)
         nc.scalar.activation(out=warm[:, 1:2], in_=warm[:, 0:1], func=ACT.Sigmoid)
 
         nc.sync.dma_start(lists[2][:], offs2)
-        nc.sync.dma_start(lists[3][:], offs3)
-        nc.sync.dma_start(lists[1][:], offs)
         for q in range(4):
             nc.sync.dma_start(
                 out=tab_plane[32 * q : 32 * q + 8, :].bitcast(I32),
                 in_=tab_scales[:, 4 * q : 4 * q + 4, :].bitcast(I32),
             )
+        nc.sync.dma_start(lists[3][:], offs3)
+        nc.sync.dma_start(lists[1][:], offs)
         w1_raw = [keep.tile([P, 4, H], F32, name="w1_raw%d" % a) for a in range(PASSES)]
         nc.sync.dma_start(out=w1_raw[0][:], in_=w1[0:512, :].rearrange("(p i) c -> p i c", i=4))
         for q in range(4):
@@ -92,6 +92,9 @@ def tile_list_polypharmacy_triple_risk_kernel(
             for e in range(4):
                 nc.sync.dma_start(out=gain_sb[e:P:4, :], in_=gain.rearrange("(u t e) -> e u t", t=4, e=4)[e])
             nc.sync.dma_start(out=b_sb[:], in_=b.rearrange("(g p) -> p g", p=P))
+
+        gain_rep = keep.tile([P, UNIT, 4], F32)
+        nc.scalar.copy(out=gain_rep[:], in_=gain_sb[:].unsqueeze(1).to_broadcast([P, UNIT, 4]))
 
         w1_codes = keep.tile([P, PASSES, H], U32, align_bytes=64)
         w1_planes = keep.tile([P, PASSES, H], U8, align_bytes=64)
@@ -163,12 +166,15 @@ def tile_list_polypharmacy_triple_risk_kernel(
                         start=(a == 0),
                         stop=(a == PASSES - 1),
                     )
-            if c == CHUNKS - 1:
+            if woven(unit):
                 return bank[:].rearrange("p t j -> p j t")
             return bank[:]
 
-        def shaped(flat, c):
-            if c == CHUNKS - 1:
+        def woven(unit):
+            return unit % 2 == 0 or unit == 2 * CHUNKS - 1
+
+        def shaped(flat, unit):
+            if woven(unit):
                 return flat[:].rearrange("p (j t) -> p j t", t=4)
             return flat[:].rearrange("p (t j) -> p t j", t=4)
 
@@ -197,65 +203,70 @@ def tile_list_polypharmacy_triple_risk_kernel(
         for a in range(PASSES):
             for role in (2, 3, 1):
                 gather(0, role, a)
-        p2_sb = {}
+        p2_sb, p23 = {}, {}
 
         def second_drug(c):
             for unit in (2 * c, 2 * c + 1):
                 p2 = project(2, unit)
                 p2_sb[unit] = ring.tile([P, 4 * UNIT], F32, name="p2_sb")
-                nc.scalar.copy(out=shaped(p2_sb[unit], c), in_=p2)
+                nc.scalar.copy(out=shaped(p2_sb[unit], unit), in_=p2)
+
+        def side_effect(c):
+            for unit in (2 * c, 2 * c + 1):
+                p3 = project(3, unit)
+                p23[unit] = ring.tile([P, 4 * UNIT], F32, name="p23")
+                if unit == 2 * CHUNKS - 1:
+                    nc.vector.tensor_tensor(
+                        out=shaped(p23[unit], unit), in0=shaped(p2_sb[unit], unit), in1=p3, op=MULT
+                    )
+                else:
+                    p3_sb = ring.tile([P, 4 * UNIT], F32, name="p3_sb")
+                    nc.scalar.copy(out=shaped(p3_sb, unit), in_=p3)
+                    nc.gpsimd.tensor_tensor(out=p23[unit][:], in0=p2_sb[unit][:], in1=p3_sb[:], op=MULT)
 
         second_drug(0)
+        side_effect(0)
         pending = None
         for c in range(CHUNKS):
             last = c == CHUNKS - 1
             units = (2 * c, 2 * c + 1)
-            p23, x = {}, {}
+            x = {}
             if not last:
                 for a in range(PASSES):
                     gather(c + 1, 2, a)
-            for unit in units:
-                p3 = project(3, unit)
-                p23[unit] = ring.tile([P, 4 * UNIT], F32, name="p23")
-                nc.vector.tensor_tensor(out=shaped(p23[unit], c), in0=shaped(p2_sb[unit], c), in1=p3, op=MULT)
-            if not last:
                 second_drug(c + 1)
                 for a in range(PASSES):
                     gather(c + 1, 3, a)
+                side_effect(c + 1)
+            for unit in units:
+                p1 = project(1, unit)
+                x[unit] = ring.tile([P, 4 * UNIT], F32, name="x")
+                nc.vector.tensor_tensor(out=shaped(x[unit], unit), in0=shaped(p23[unit], unit), in1=p1, op=MULT)
             if c == 0:
                 nc.vector.quantize_mx(out=w4_codes[:].bitcast(FP8X4), scales=w4_plane[:], in_=w4_bf[:])
             if pending is not None:
                 readout(*pending)
-            for unit in units:
-                p1 = project(1, unit)
-                x[unit] = ring.tile([P, 4 * UNIT], F32, name="x")
-                nc.vector.tensor_tensor(out=shaped(x[unit], c), in0=shaped(p23[unit], c), in1=p1, op=MULT)
             if not last:
                 for a in range(PASSES):
                     gather(c + 1, 1, a)
-                sig = ring.tile([P, 4, CHUNK], F32, name="sig")
-                for half in range(2):
-                    nc.scalar.activation(
-                        out=sig[:, :, half * UNIT : (half + 1) * UNIT], in_=shaped(x[units[half]], c), func=ACT.Sigmoid
-                    )
-                h_rows = ring.tile([P, 4, CHUNK], BF16, name="h_rows")
-                for t in range(4):
-                    nc.scalar.activation(out=h_rows[:, t, :], in_=sig[:, t, :], func=ACT.Copy, scale=gain_sb[:, t : t + 1])
-                h_bf = ring.tile([P, 4 * CHUNK], BF16, name="h_bf", align_bytes=64)
-                nc.scalar.copy(
-                    out=h_bf[:].rearrange("p (c t) -> p c t", t=4),
-                    in_=h_rows[:].rearrange("p t c -> p c t"),
-                )
-                pending = (h_bf, c)
-            else:
-                h_bf = ring.tile([P, 4 * CHUNK], BF16, name="h_bf", align_bytes=64)
-                for half in range(2):
-                    sig = ring.tile([P, UNIT, 4], F32, name="sig_last")
-                    nc.scalar.activation(out=sig[:], in_=shaped(x[units[half]], c), func=ACT.Sigmoid)
-                    nc.vector.tensor_tensor(
-                        out=h_bf[:, half * 4 * UNIT : (half + 1) * 4 * UNIT].rearrange("p (j t) -> p j t", t=4),
-                        in0=sig[:],
-                        in1=gain_sb[:].unsqueeze(1).to_broadcast([P, UNIT, 4]),
-                        op=MULT,
-                    )
-                readout(h_bf, c)
+            h_bf = ring.tile([P, 4 * CHUNK], BF16, name="h_bf", align_bytes=64)
+            for half in range(2):
+                unit = units[half]
+                h_part = h_bf[:, half * 4 * UNIT : (half + 1) * 4 * UNIT]
+                sig = ring.tile([P, 4 * UNIT], F32, name="sig")
+                nc.scalar.activation(out=sig[:], in_=x[unit][:], func=ACT.Sigmoid)
+                if woven(unit):
+                    engine = nc.vector if last else nc.gpsimd
+                    engine.tensor_tensor(out=h_part, in0=sig[:], in1=gain_rep[:].rearrange("p j t -> p (j t)"), op=MULT)
+                else:
+                    h_rows = ring.tile([P, 4, UNIT], BF16, name="h_rows")
+                    for t in range(4):
+                        nc.scalar.activation(
+                            out=h_rows[:, t, :],
+                            in_=sig[:, t * UNIT : (t + 1) * UNIT],
+                            func=ACT.Copy,
+                            scale=gain_sb[:, t : t + 1],
+                        )
+                    nc.scalar.copy(out=h_part.rearrange("p (j t) -> p j t", t=4), in_=h_rows[:].rearrange("p t j -> p j t"))
+            pending = (h_bf, c)
+        readout(*pending)

from contextlib import ExitStack

import concourse.mybir as mybir

K, T, S, H, N = 1024, 2048, 1024, 512, 256
FLOPS = 2 * 3 * K * H * S + 2 * H * N * S

F32 = mybir.dt.float32
BF16 = mybir.dt.bfloat16
I32 = mybir.dt.int32
U32 = mybir.dt.uint32
U16 = mybir.dt.uint16
U8 = mybir.dt.uint8
FP8X4 = mybir.dt.float8_e4m3fn_x4
FP4X4 = mybir.dt.float4_e2m1fn_x4
ACT = mybir.ActivationFunctionType
MULT = mybir.AluOpType.mult

P = 128
PASSES = 2
UNIT = 128
CHUNK = 256
CHUNKS = S // CHUNK


def tile_list_polypharmacy_triple_risk_kernel(
    tc, tab_words, tab_scales, offs, offs2, offs3, w1, w2_words, w2_scales, w3_words, w3_scales, gain, w4, b, out
):
    nc = tc.nc
    with ExitStack() as ctx:
        keep = ctx.enter_context(tc.tile_pool(name="keep", bufs=1))
        ring = ctx.enter_context(tc.tile_pool(name="ring", bufs=2))
        psum = ctx.enter_context(tc.psum_pool(name="psum", bufs=2))

        lists = {}
        for role in (2, 3, 1):
            lists[role] = keep.tile([P, S // 16], U16, name="list%d" % role)
        tab_plane = keep.tile([P, T], U8, align_bytes=64)
        w_planes_raw = keep.tile([P, 3, H], U8, align_bytes=64)
        v3_plane1 = keep.tile([P, S], U8, align_bytes=64)
        warm = keep.tile([P, 2], F32)

        nc.gpsimd.memset(tab_plane[:].bitcast(I32), 0)
        nc.gpsimd.memset(w_planes_raw[:].rearrange("p s c -> p (s c)").bitcast(I32), 0)
        nc.gpsimd.memset(v3_plane1[:].bitcast(I32), 0)
        nc.gpsimd.memset(warm[:, 0:1], 0.0)
        nc.scalar.activation(out=warm[:, 1:2], in_=warm[:, 0:1], func=ACT.Sigmoid)

        nc.sync.dma_start(lists[2][:], offs2)
        for q in range(4):
            nc.sync.dma_start(
                out=tab_plane[32 * q : 32 * q + 8, :].bitcast(I32),
                in_=tab_scales[:, 4 * q : 4 * q + 4, :].bitcast(I32),
            )
        nc.sync.dma_start(lists[3][:], offs3)
        nc.sync.dma_start(lists[1][:], offs)
        w1_raw = [keep.tile([P, 4, H], F32, name="w1_raw%d" % a) for a in range(PASSES)]
        nc.sync.dma_start(out=w1_raw[0][:], in_=w1[0:512, :].rearrange("(p i) c -> p i c", i=4))
        for q in range(4):
            nc.sync.dma_start(
                out=w_planes_raw[32 * q : 32 * q + 8, 0, :].bitcast(I32),
                in_=w2_scales[:, 4 * q : 4 * q + 4, :].bitcast(I32),
            )
        nc.sync.dma_start(out=w1_raw[1][:], in_=w1[512:1024, :].rearrange("(p i) c -> p i c", i=4))
        w2_raw = keep.tile([P, PASSES, H], I32)
        nc.sync.dma_start(out=w2_raw[:], in_=w2_words.rearrange("a p c i -> p a (c i)").bitcast(I32))
        w3_raw = keep.tile([P, PASSES, H // 2], I32)
        nc.sync.dma_start(out=w3_raw[:], in_=w3_words.rearrange("a p c -> p a c").bitcast(I32))
        for q in range(4):
            nc.sync.dma_start(
                out=w_planes_raw[32 * q : 32 * q + 4, 1:3, :].bitcast(I32),
                in_=w3_scales[:, 4 * q : 4 * q + 4, :].rearrange("a r c -> r a c").bitcast(I32),
            )
        tab = [keep.tile([P, T], I32, name="tab%d" % a, align_bytes=64) for a in range(PASSES)]
        for a in range(PASSES):
            nc.sync.dma_start(out=tab[a][:], in_=tab_words[a].rearrange("p t i -> p (t i)").bitcast(I32))

        v_plane = {}
        for role in (2, 3, 1):
            v_plane[role] = keep.tile([P, S], U8, name="v_plane%d" % role, align_bytes=64)
            nc.vector.tensor_copy(v_plane[role][:], tab_plane[:].indirect(lists[role][:]))
            if role == 3:
                nc.sync.dma_start(out=v3_plane1[0 : P - 4, :].bitcast(I32), in_=v_plane[3][4:P, :].bitcast(I32))

        w4_raw = keep.tile([P, 4, N], F32)
        w4_rows = w4.rearrange("(u t e) n -> t u e n", t=4, e=4)
        for t in range(4):
            nc.sync.dma_start(out=w4_raw[:, t, :], in_=w4_rows[t])
        gain_sb = keep.tile([P, 4], F32)
        b_sb = keep.tile([P, 2], F32)
        with nc.allow_non_contiguous_dma(reason="one value of a short vector for each partition"):
            for e in range(4):
                nc.sync.dma_start(out=gain_sb[e:P:4, :], in_=gain.rearrange("(u t e) -> e u t", t=4, e=4)[e])
            nc.sync.dma_start(out=b_sb[:], in_=b.rearrange("(g p) -> p g", p=P))

        gain_rep = keep.tile([P, UNIT, 4], F32)
        nc.scalar.copy(out=gain_rep[:], in_=gain_sb[:].unsqueeze(1).to_broadcast([P, UNIT, 4]))

        w1_codes = keep.tile([P, PASSES, H], U32, align_bytes=64)
        w1_planes = keep.tile([P, PASSES, H], U8, align_bytes=64)
        for a in range(PASSES):
            w1_bf = keep.tile([P, 4 * H], BF16, name="w1_bf%d" % a, align_bytes=64)
            nc.scalar.copy(
                out=w1_bf[:].rearrange("p (t u e i) -> p t u e i", t=4, e=4, i=4),
                in_=w1_raw[a][:].rearrange("p i (u t e) -> p t u e i", t=4, e=4),
            )
            nc.vector.quantize_mx(out=w1_codes[:, a, :].bitcast(FP8X4), scales=w1_planes[:, a, :], in_=w1_bf[:])

        w2_codes = keep.tile([P, PASSES, H], I32, align_bytes=64)
        nc.vector.tensor_copy(
            out=w2_codes[:].rearrange("p a (t u e) -> p a t u e", t=4, e=4),
            in_=w2_raw[:].rearrange("p a (u t e) -> p a t u e", t=4, e=4),
        )
        w3_codes = keep.tile([P, PASSES, H // 2], I32, align_bytes=64)
        nc.vector.tensor_copy(
            out=w3_codes[:].rearrange("p a (t u e) -> p a t u e", t=4, e=2),
            in_=w3_raw[:].rearrange("p a (u t e) -> p a t u e", t=4, e=2),
        )
        w_planes = keep.tile([P, 3, H], U8, align_bytes=64)
        nc.vector.tensor_copy(
            out=w_planes[:].bitcast(I32).rearrange("p s (t u) -> p s t u", t=4),
            in_=w_planes_raw[:].bitcast(I32).rearrange("p s (u t) -> p s t u", t=4),
        )

        w4_bf = keep.tile([P, 4 * N], BF16, align_bytes=64)
        nc.scalar.copy(
            out=w4_bf[:].rearrange("p (c t) -> p c t", t=4),
            in_=w4_raw[:].rearrange("p t c -> p c t"),
        )
        w4_codes = keep.tile([P, N], U32, align_bytes=64)
        w4_plane = keep.tile([P, N], U8, align_bytes=64)

        def stationary(role, a, t):
            cols = slice(P * t, P * t + P)
            if role == 1:
                return w1_codes[:, a, cols].bitcast(FP8X4), w1_planes[:, a, cols]
            if role == 2:
                return w2_codes[:, a, cols].bitcast(FP8X4), w_planes[4 * a : P, 0, cols]
            return w3_codes[:, a, 64 * t : 64 * t + 64].bitcast(FP4X4), w_planes[:, 1 + a, cols]

        def moving_plane(role, a, cols):
            if role == 3 and a == 1:
                return v3_plane1[:, cols]
            return v_plane[role][4 * a : P, cols]

        words = {}

        def gather(c, role, a):
            g = keep.tile([P, CHUNK], U32, name="g%d%d" % (role, a), align_bytes=64)
            part = lists[role][:, c * CHUNK // 16 : (c + 1) * CHUNK // 16]
            nc.vector.tensor_copy(g[:], tab[a][:].bitcast(U32).indirect(part))
            words[(c, role, a)] = g

        def project(role, unit):
            c, half = divmod(unit, 2)
            bank = psum.tile([P, 4, UNIT], F32, name="p%d" % role)
            for t in range(4):
                for a in range(PASSES):
                    codes, plane = stationary(role, a, t)
                    nc.tensor.matmul_mx(
                        out=bank[:, t, :],
                        lhsT=codes,
                        lhsT_scale=plane,
                        rhs=words[(c, role, a)][:, half * UNIT : (half + 1) * UNIT].bitcast(FP8X4),
                        rhs_scale=moving_plane(role, a, slice(unit * UNIT, (unit + 1) * UNIT)),
                        start=(a == 0),
                        stop=(a == PASSES - 1),
                    )
            if woven(unit):
                return bank[:].rearrange("p t j -> p j t")
            return bank[:]

        def woven(unit):
            return unit % 2 == 0 or unit == 2 * CHUNKS - 1

        def shaped(flat, unit):
            if woven(unit):
                return flat[:].rearrange("p (j t) -> p j t", t=4)
            return flat[:].rearrange("p (t j) -> p t j", t=4)

        def readout(h_bf, c):
            h_codes = ring.tile([P, CHUNK], U32, name="h_codes", align_bytes=64)
            h_plane = ring.tile([P, CHUNK], U8, name="h_plane", align_bytes=64)
            nc.vector.quantize_mx(out=h_codes[:].bitcast(FP8X4), scales=h_plane[:], in_=h_bf[:])
            for g in range(2):
                y = psum.tile([P, CHUNK], F32, name="y")
                nc.tensor.matmul_mx(
                    out=y[:],
                    lhsT=w4_codes[:, g * P : (g + 1) * P].bitcast(FP8X4),
                    lhsT_scale=w4_plane[:, g * P : (g + 1) * P],
                    rhs=h_codes[:].bitcast(FP8X4),
                    rhs_scale=h_plane[:],
                    start=True,
                    stop=True,
                )
                res = ring.tile([P, CHUNK], F32, name="res%d" % g)
                if c == CHUNKS - 1 and g == 1:
                    nc.vector.tensor_scalar_add(out=res[:], in0=y[:], scalar1=b_sb[:, g : g + 1])
                else:
                    nc.scalar.activation(out=res[:], in_=y[:], func=ACT.Identity, bias=b_sb[:, g : g + 1])
                nc.sync.dma_start(out=out[g * P : (g + 1) * P, c * CHUNK : (c + 1) * CHUNK], in_=res[:])

        for a in range(PASSES):
            for role in (2, 3, 1):
                gather(0, role, a)
        p2_sb, p23 = {}, {}

        def second_drug(c):
            for unit in (2 * c, 2 * c + 1):
                p2 = project(2, unit)
                p2_sb[unit] = ring.tile([P, 4 * UNIT], F32, name="p2_sb")
                nc.scalar.copy(out=shaped(p2_sb[unit], unit), in_=p2)

        def side_effect(c):
            for unit in (2 * c, 2 * c + 1):
                p3 = project(3, unit)
                p23[unit] = ring.tile([P, 4 * UNIT], F32, name="p23")
                if unit == 2 * CHUNKS - 1:
                    nc.vector.tensor_tensor(
                        out=shaped(p23[unit], unit), in0=shaped(p2_sb[unit], unit), in1=p3, op=MULT
                    )
                else:
                    p3_sb = ring.tile([P, 4 * UNIT], F32, name="p3_sb")
                    nc.scalar.copy(out=shaped(p3_sb, unit), in_=p3)
                    nc.gpsimd.tensor_tensor(out=p23[unit][:], in0=p2_sb[unit][:], in1=p3_sb[:], op=MULT)

        second_drug(0)
        side_effect(0)
        pending = None
        for c in range(CHUNKS):
            last = c == CHUNKS - 1
            units = (2 * c, 2 * c + 1)
            x = {}
            if not last:
                for a in range(PASSES):
                    gather(c + 1, 2, a)
                second_drug(c + 1)
                for a in range(PASSES):
                    gather(c + 1, 3, a)
                side_effect(c + 1)
            for unit in units:
                p1 = project(1, unit)
                x[unit] = ring.tile([P, 4 * UNIT], F32, name="x")
                nc.vector.tensor_tensor(out=shaped(x[unit], unit), in0=shaped(p23[unit], unit), in1=p1, op=MULT)
            if c == 0:
                nc.vector.quantize_mx(out=w4_codes[:].bitcast(FP8X4), scales=w4_plane[:], in_=w4_bf[:])
            if pending is not None:
                readout(*pending)
            if not last:
                for a in range(PASSES):
                    gather(c + 1, 1, a)
            h_bf = ring.tile([P, 4 * CHUNK], BF16, name="h_bf", align_bytes=64)
            for half in range(2):
                unit = units[half]
                h_part = h_bf[:, half * 4 * UNIT : (half + 1) * 4 * UNIT]
                sig = ring.tile([P, 4 * UNIT], F32, name="sig")
                nc.scalar.activation(out=sig[:], in_=x[unit][:], func=ACT.Sigmoid)
                if woven(unit):
                    engine = nc.vector if last else nc.gpsimd
                    engine.tensor_tensor(out=h_part, in0=sig[:], in1=gain_rep[:].rearrange("p j t -> p (j t)"), op=MULT)
                else:
                    h_rows = ring.tile([P, 4, UNIT], BF16, name="h_rows")
                    for t in range(4):
                        nc.scalar.activation(
                            out=h_rows[:, t, :],
                            in_=sig[:, t * UNIT : (t + 1) * UNIT],
                            func=ACT.Copy,
                            scale=gain_sb[:, t : t + 1],
                        )
                    nc.scalar.copy(out=h_part.rearrange("p (j t) -> p j t", t=4), in_=h_rows[:].rearrange("p t j -> p j t"))
            pending = (h_bf, c)
        readout(*pending)
